import numpy as np
import ml_dtypes


def mxq(x, axis, fmt="e4m3"):
    dtype, down = {"e4m3": (ml_dtypes.float8_e4m3fn, 7), "e5m2": (ml_dtypes.float8_e5m2, 14)}[fmt]
    v = np.moveaxis(np.asarray(x, np.float32).astype(ml_dtypes.bfloat16).astype(np.float64), axis, -1)
    blocks = v.reshape(v.shape[:-1] + (-1, 32))
    amax = np.abs(blocks).max(-1, keepdims=True)
    byte = np.maximum(np.where(amax > 0, np.frexp(amax)[1] - 1 + 127, 0) - down, 1)
    scale = np.exp2(byte - 127.0)
    codes = (blocks / scale).astype(np.float32).astype(dtype).astype(np.float64)
    return np.moveaxis((codes * scale).reshape(v.shape), -1, axis)


WIDE = False


def mx_kscale(k):
    if not WIDE:
        return np.ones(k)
    levels = np.array([10, -10, 5, -5, 0])
    if k % 512:
        return np.exp2(np.random.permutation(np.resize(levels, k // 32))).repeat(32)
    a = np.empty((k // 512, 16))
    for p in range(k // 512):
        a[p, :8] = np.random.permutation(np.resize(levels, 8))
        for g in range(8):
            far = levels[np.abs(levels - a[p, g]) >= 10]
            a[p, g + 8] = far[np.random.randint(len(far))]
    return np.exp2(a.ravel()).repeat(32)


def f64(x):
    return np.asarray(x).astype(np.float64)


def striped(idx):
    return np.tile(idx.reshape(-1, 16).T, (8, 1)).astype(np.uint16)


def unstriped(offs):
    return offs[:16].T.reshape(-1).astype(np.int64)


def relu2(v):
    return np.maximum(v, 0.0) ** 2


K, T, E, C, H, N = 2560, 640, 2, 256, 512, 384


def by_expert(wq, xq):
    return np.concatenate([wq[e].T @ xq[:, e * C:(e + 1) * C] for e in range(E)], axis=1)


def setup_inputs():
    n = np.random.standard_normal
    s = mx_kscale(K)[:, None]
    u = mx_kscale(H)
    return {
        "xT": (n((K, T)) * s).astype(np.float32),
        "w1": (n((E, K, H)) / np.sqrt(K) / s[None] * u[None, None, :]).astype(np.float32),
        "w2": (n((E, H, N)) / np.sqrt(H) / u[None, :, None] ** 2).astype(np.float32),
        "gate": np.tile(np.random.uniform(0.2, 1.0, E * C), (K, 1)).astype(np.float32),
        "offs": striped(np.random.permutation(T)[:E * C]),
    }


def reference(xT, w1, w2, gate, offs):
    idx = unstriped(offs)
    xq = mxq(f64(gate) * f64(xT)[:, idx], 0, "e4m3")
    h = relu2(by_expert(mxq(f64(w1), 1, "e4m3"), xq))
    y = by_expert(mxq(f64(w2), 1, "e4m3"), mxq(h, 0, "e4m3"))
    out = np.zeros((N, T))
    out[:, idx] = y
    return out

@@ -1,0 +1,243 @@
+from contextlib import ExitStack
+
+import concourse.mybir as mybir
+
+K, T, E, C, H, N = 2560, 640, 2, 256, 512, 384
+FLOPS = 2 * E * C * (K * H + H * N)
+BYTES = 4 * (K * T + E * K * H + E * H * N + E * C + N * T) + 2 * 128 * (E * C // 16)
+
+F32 = mybir.dt.float32
+BF16 = mybir.dt.bfloat16
+U32 = mybir.dt.uint32
+U16 = mybir.dt.uint16
+U8 = mybir.dt.uint8
+FP8X4 = mybir.dt.float8_e4m3fn_x4
+ACT = mybir.ActivationFunctionType
+ALU = mybir.AluOpType
+
+P = 128
+PACK = 4
+K_PASS = P * PACK
+PASSES = K // K_PASS
+HALF = C // 2
+N_BLOCKS = N // P
+PER_COL = 16
+SHARED = 2
+
+
+def tile_moe_pre_mlp_relu2_kernel(tc, xT, w1, w2, gate, offs, out):
+    nc = tc.nc
+    with ExitStack() as ctx:
+        keep = ctx.enter_context(tc.tile_pool(name="keep", bufs=1))
+        ring = ctx.enter_context(tc.tile_pool(name="ring", bufs=3))
+        psum = ctx.enter_context(tc.psum_pool(name="psum", bufs=1))
+
+        offsets = keep.tile([P, E * C // PER_COL], U16, name="offsets")
+        gate_sb = keep.tile([P, E * C], F32, name="gate_sb")
+        x_rows = [[keep.tile([P, T], F32, name=f"x_row{g}_{j}") for j in range(PACK)] for g in range(SHARED)]
+        x_raw = [keep.tile([P, PACK * T], F32, name=f"x_raw{g}") for g in range(SHARED, PASSES)]
+        w1_raw = [[keep.tile([P, PACK * H], F32, name=f"w1_raw{e}_{g}") for g in range(PASSES)] for e in range(E)]
+        w2_raw = [keep.tile([P, PACK * N], F32, name=f"w2_raw{e}") for e in range(E)]
+        windows = [keep.tile([P, T], F32, name=f"window{b}") for b in range(N_BLOCKS)]
+        gathered = [keep.tile([P, PACK * C], F32, name=f"gathered{i}") for i in range(3)]
+        gated = keep.tile([P, PACK * C], F32, name="gated")
+        stage = [keep.tile([P, PACK * H], BF16, name=f"stage{i}", align_bytes=64) for i in range(2)]
+        w2_bf = keep.tile([P, PACK * N], BF16, name="w2_bf", align_bytes=64)
+
+        def load_rows(dst, rows):
+            nc.sync.dma_start(out=dst[:], in_=rows.rearrange("(p j) w -> p (j w)", j=PACK))
+
+        def load_x_row(g, j):
+            rows = xT[g * K_PASS:(g + 1) * K_PASS, :].rearrange("(p j) w -> p j w", j=PACK)
+            nc.sync.dma_start(out=x_rows[g][j][:], in_=rows[:, j, :])
+
+        def load_x(g):
+            load_rows(x_raw[g - SHARED], xT[g * K_PASS:(g + 1) * K_PASS, :])
+
+        def load_w1(e, g):
+            load_rows(w1_raw[e][g], w1[e, g * K_PASS:(g + 1) * K_PASS, :])
+
+        def x_window(g, j):
+            if g < SHARED:
+                return x_rows[g][j][:]
+            return x_raw[g - SHARED][:, j * T:(j + 1) * T]
+
+        nc.sync.dma_start(offsets[:], offs)
+        load_x_row(0, 0)
+        nc.sync.dma_start(out=gate_sb[:], in_=gate[0:P, :])
+        for g in range(SHARED):
+            for j in range(PACK):
+                if g + j > 0:
+                    load_x_row(g, j)
+        for g in range(SHARED, PASSES):
+            load_x(g)
+            load_w1(0, g - SHARED)
+        for g in range(PASSES - SHARED, PASSES):
+            load_w1(0, g)
+        load_rows(w2_raw[0], w2[0])
+        load_w1(1, 0)
+        load_rows(w2_raw[1], w2[1])
+        for g in range(1, PASSES):
+            load_w1(1, g)
+
+        nc.gpsimd.memset(windows[0][:], 0.0)
+        nc.scalar.activation(windows[1][:], windows[0][:], ACT.Copy)
+        nc.gpsimd.memset(windows[2][:], 0.0)
+
+        def slots(e, first=0, count=C):
+            start = (e * C + first) // PER_COL
+            return offsets[:, start:start + count // PER_COL]
+
+        def quantize(values, width, name, pool=keep):
+            codes = pool.tile([P, width], U32, name=f"{name}_codes", align_bytes=64)
+            scales = pool.tile([P, width], U8, name=f"{name}_scales", align_bytes=64)
+            nc.vector.quantize_mx(out=codes[:].bitcast(FP8X4), scales=scales[:], in_=values[:, :])
+            return codes, scales
+
+        def pairs(ap, order):
+            return ap.rearrange(f"p ({order}) -> p c j i", i=2, j=PACK)
+
+        def gather(e, g, dst):
+            for j in range(PACK):
+                nc.scalar.activation(dst[:, j * C:(j + 1) * C], x_window(g, j).indirect(slots(e)), ACT.Copy)
+
+        def gate_and_weave(e, src, dst):
+            weight = gate_sb[:, e * C:(e + 1) * C].rearrange("p (c i) -> p c i", i=2)
+            nc.vector.tensor_tensor(
+                pairs(dst[:, 0:C * PACK], "c i j"),
+                pairs(src[:], "j c i"),
+                weight.unsqueeze(2).to_broadcast([P, C // 2, PACK, 2]),
+                ALU.mult,
+            )
+
+        def gather_gated(e, g, dst):
+            for j in range(PACK):
+                nc.vector.tensor_tensor(
+                    gated[:, j * C:(j + 1) * C], x_window(g, j).indirect(slots(e)), gate_sb[:, e * C:(e + 1) * C], ALU.mult
+                )
+            nc.vector.tensor_copy(pairs(dst[:, 0:C * PACK], "c i j"), pairs(gated[:], "j c i"))
+
+        def weave_w1(e, g, dst, split):
+            to = dst[:].rearrange("p (u i m j) -> p u m j i", u=2, i=2, j=PACK)
+            fro = w1_raw[e][g][:].rearrange("p (j m u i) -> p u m j i", u=2, i=2, j=PACK)
+            if split > 0:
+                nc.vector.tensor_copy(to[:, :, 0:split], fro[:, :, 0:split])
+            if split < P:
+                nc.scalar.copy(to[:, :, split:P], fro[:, :, split:P])
+
+        def second_weights(e):
+            nc.scalar.copy(pairs(w2_bf[:], "c i j"), pairs(w2_raw[e][:], "j c i"))
+
+        def first_product(banks, g, w_q, x_q):
+            for half in range(2):
+                for t in range(PACK):
+                    nc.tensor.matmul_mx(
+                        out=banks[half][:, t * HALF:(t + 1) * HALF],
+                        lhsT=w_q[0][:, t * P:(t + 1) * P].bitcast(FP8X4),
+                        lhsT_scale=w_q[1][:, t * P:(t + 1) * P],
+                        rhs=x_q[0][:, half * HALF:(half + 1) * HALF].bitcast(FP8X4),
+                        rhs_scale=x_q[1][:, half * HALF:(half + 1) * HALF],
+                        start=(g == 0 and t == 0),
+                        stop=(g == PASSES - 1 and t == PACK - 1),
+                    )
+
+        def hidden(bank, on_scalar, name):
+            positive = ring.tile([P, HALF * PACK], F32, name="positive")
+            h_bf = ring.tile([P, HALF * PACK], BF16, name="h_bf", align_bytes=64)
+            src = bank[:].rearrange("p (t c) -> p c t", t=PACK)
+            dst = positive[:].rearrange("p (c t) -> p c t", t=PACK)
+            if on_scalar:
+                nc.scalar.activation(dst, src, ACT.Relu)
+                nc.scalar.activation(h_bf[:], positive[:], ACT.Square)
+            else:
+                nc.vector.tensor_scalar(dst, src, 0.0, None, ALU.max)
+                nc.vector.tensor_tensor(h_bf[:], positive[:], positive[:], ALU.mult)
+            return quantize(h_bf, HALF, name)
+
+        def second_product(bank, w_q, h_q, y, half, on_scalar):
+            for b in range(N_BLOCKS):
+                nc.tensor.matmul_mx(
+                    out=bank[:, b * HALF:(b + 1) * HALF],
+                    lhsT=w_q[0][:, b * P:(b + 1) * P].bitcast(FP8X4),
+                    lhsT_scale=w_q[1][:, b * P:(b + 1) * P],
+                    rhs=h_q[0][:].bitcast(FP8X4),
+                    rhs_scale=h_q[1][:],
+                    start=True,
+                    stop=True,
+                )
+            dst = y[:].rearrange("p (b c) -> p b c", b=N_BLOCKS)[:, :, half * HALF:(half + 1) * HALF]
+            src = bank[:].rearrange("p (b c) -> p b c", b=N_BLOCKS)
+            if on_scalar:
+                nc.scalar.copy(dst, src)
+            else:
+                nc.vector.tensor_copy(dst, src)
+
+        def scatter(y, e, b, first, count, on_scalar):
+            target = windows[b][:].indirect(slots(e, first, count))
+            values = y[:, b * C + first:b * C + first + count]
+            if on_scalar:
+                nc.scalar.activation(target, values, ACT.Copy)
+            else:
+                nc.vector.tensor_copy(target, values)
+
+        a_banks = [[psum.tile([P, PACK * HALF], F32, name=f"a{e}_{h}") for h in range(2)] for e in range(E)]
+        y_banks = [[psum.tile([P, N_BLOCKS * HALF], F32, name=f"yb{e}_{h}") for h in range(2)] for e in range(E)]
+        ys = [keep.tile([P, N_BLOCKS * C], F32, name=f"y{e}") for e in range(E)]
+
+        x_q = {}
+        w2_q = {}
+        h_q = {}
+        on_scalar = [(e, g) for g in range(PASSES) for e in range(E) if not (g < SHARED and e == 1)]
+        for i in range(2):
+            gather(on_scalar[i][0], on_scalar[i][1], gathered[i])
+
+        def finish(step, i):
+            kind, e, g = step
+            if kind == "x":
+                x_q[e, g] = quantize(stage[i % 2][:, 0:C * PACK], C, f"x{e}_{g}")
+            else:
+                first_product(a_banks[e], g, quantize(stage[i % 2], H, "w1", ring), x_q[e, g])
+
+        def expert_zero_hidden():
+            second_weights(0)
+            w2_q[0] = quantize(w2_bf, N, "w20")
+            for h in range(2):
+                h_q[0, h] = hidden(a_banks[0][h], True, f"h0_{h}")
+            for h in range(2):
+                second_product(y_banks[0][h], w2_q[0], h_q[0, h], ys[0], h, True)
+            second_weights(1)
+            w2_q[1] = quantize(w2_bf, N, "w21")
+            for b in range(N_BLOCKS):
+                scatter(ys[0], 0, b, 0, C, True)
+
+        steps = [("x", 1, 0), ("x", 0, 0), ("x", 1, 1), ("x", 0, 1), ("w", 0, 0), ("x", 0, 2), ("x", 1, 2), ("w", 0, 1),
+                 ("x", 0, 3), ("x", 1, 3), ("w", 0, 2), ("x", 0, 4), ("w", 0, 3), ("w", 0, 4), ("x", 1, 4),
+                 ("w", 1, 0), ("w", 1, 1), ("w", 1, 2), ("w", 1, 3), ("w", 1, 4)]
+        for i, step in enumerate(steps):
+            kind, e, g = step
+            dst = stage[i % 2]
+            if kind == "w":
+                weave_w1(e, g, dst, {(0, 4): 0, (1, 4): 88}.get((e, g), P))
+            elif (e, g) in on_scalar:
+                n = on_scalar.index((e, g))
+                gate_and_weave(e, gathered[n % 3], dst)
+                if n + 2 < len(on_scalar):
+                    gather(on_scalar[n + 2][0], on_scalar[n + 2][1], gathered[(n + 2) % 3])
+            else:
+                gather_gated(e, g, dst)
+            if i > 0:
+                finish(steps[i - 1], i - 1)
+            if step == ("w", 1, 0):
+                expert_zero_hidden()
+        finish(steps[-1], len(steps) - 1)
+
+        for h in range(2):
+            h_q[1, h] = hidden(a_banks[1][h], h == 0, f"h1_{h}")
+        for h in range(2):
+            second_product(y_banks[1][h], w2_q[1], h_q[1, h], ys[1], h, h == 0)
+        scatter(ys[1], 1, 2, 0, HALF, True)
+        scatter(ys[1], 1, 0, 0, C, False)
+        scatter(ys[1], 1, 1, 0, C, True)
+        scatter(ys[1], 1, 2, HALF, HALF, False)
+        for b in range(N_BLOCKS):
+            nc.sync.dma_start(out=out[b * P:(b + 1) * P, :], in_=windows[b][:])

@@ -23,6 +23,19 @@ HALF = C // 2
 N_BLOCKS = N // P
 PER_COL = 16
 SHARED = 2
+PLANES = 3
+LOADS = [("x", 3), ("w", 0), ("x", 4), ("w", 1), ("w", 2), ("w", 3), ("w", 4)]
+LEAD = 1
+W1_TILES = 8
+ON_S = {(0, 3): 0, (0, 4): 1}
+H0S = [True, True]
+Y0S = [True, True]
+SC0V = 0
+LAST = 128
+W2L = 32
+STEPS = [("x", 0, 0), ("x", 0, 1), ("x", 0, 2), ("w", 0, 0), ("x", 0, 3), ("w", 0, 1), ("x", 0, 4), ("w", 0, 2), ("x", 1, 4), ("w", 0, 3), ("w", 0, 4), ("w", 1, 0), ("w", 1, 1), ("w", 1, 2), ("w", 1, 3), ("w", 1, 4)]
+S = E * C
+WIDE = 2 * S
 
 
 def tile_moe_pre_mlp_relu2_kernel(tc, xT, w1, w2, gate, offs, out):
@@ -34,55 +47,52 @@ def tile_moe_pre_mlp_relu2_kernel(tc, xT, w1, w2, gate, offs, out):
 
         offsets = keep.tile([P, E * C // PER_COL], U16, name="offsets")
         gate_sb = keep.tile([P, E * C], F32, name="gate_sb")
-        x_rows = [[keep.tile([P, T], F32, name=f"x_row{g}_{j}") for j in range(PACK)] for g in range(SHARED)]
-        x_raw = [keep.tile([P, PACK * T], F32, name=f"x_raw{g}") for g in range(SHARED, PASSES)]
-        w1_raw = [[keep.tile([P, PACK * H], F32, name=f"w1_raw{e}_{g}") for g in range(PASSES)] for e in range(E)]
+        x_rows = [[keep.tile([P, T], F32, name=f"x_row{g}_{j}") for j in range(PACK)] for g in range(PLANES)]
+        x_raw = [keep.tile([P, (PACK - 1) * T + WIDE], F32, name=f"x_raw{g}") for g in range(PLANES, PASSES)]
+        w1_tiles = [keep.tile([P, PACK * H], F32, name=f"w1_raw{i}") for i in range(W1_TILES)]
+        w1_raw = [[w1_tiles[(e * PASSES + g) % W1_TILES] for g in range(PASSES)] for e in range(E)]
         w2_raw = [keep.tile([P, PACK * N], F32, name=f"w2_raw{e}") for e in range(E)]
         windows = [keep.tile([P, T], F32, name=f"window{b}") for b in range(N_BLOCKS)]
-        gathered = [keep.tile([P, PACK * C], F32, name=f"gathered{i}") for i in range(3)]
+        gathered = [keep.tile([P, PACK * S], F32, name=f"gathered{i}") for i in range(2)]
         gated = keep.tile([P, PACK * C], F32, name="gated")
         stage = [keep.tile([P, PACK * H], BF16, name=f"stage{i}", align_bytes=64) for i in range(2)]
+        side = [keep.tile([P, PACK * H], BF16, name=f"side{i}", align_bytes=64) for i in range(2)]
         w2_bf = keep.tile([P, PACK * N], BF16, name="w2_bf", align_bytes=64)
 
         def load_rows(dst, rows):
-            nc.sync.dma_start(out=dst[:], in_=rows.rearrange("(p j) w -> p (j w)", j=PACK))
+            nc.sync.dma_start(out=dst[:, :], in_=rows.rearrange("(p j) w -> p (j w)", j=PACK))
 
         def load_x_row(g, j):
             rows = xT[g * K_PASS:(g + 1) * K_PASS, :].rearrange("(p j) w -> p j w", j=PACK)
             nc.sync.dma_start(out=x_rows[g][j][:], in_=rows[:, j, :])
 
         def load_x(g):
-            load_rows(x_raw[g - SHARED], xT[g * K_PASS:(g + 1) * K_PASS, :])
+            load_rows(x_raw[g - PLANES][:, 0:PACK * T], xT[g * K_PASS:(g + 1) * K_PASS, :])
 
         def load_w1(e, g):
             load_rows(w1_raw[e][g], w1[e, g * K_PASS:(g + 1) * K_PASS, :])
 
-        def x_window(g, j):
-            if g < SHARED:
-                return x_rows[g][j][:]
-            return x_raw[g - SHARED][:, j * T:(j + 1) * T]
-
         nc.sync.dma_start(offsets[:], offs)
         load_x_row(0, 0)
         nc.sync.dma_start(out=gate_sb[:], in_=gate[0:P, :])
-        for g in range(SHARED):
+        for g in range(PLANES):
             for j in range(PACK):
                 if g + j > 0:
                     load_x_row(g, j)
-        for g in range(SHARED, PASSES):
-            load_x(g)
-            load_w1(0, g - SHARED)
-        for g in range(PASSES - SHARED, PASSES):
-            load_w1(0, g)
+        for kind, g in LOADS:
+            if kind == "x":
+                load_x(g)
+            else:
+                load_w1(0, g)
         load_rows(w2_raw[0], w2[0])
-        load_w1(1, 0)
-        load_rows(w2_raw[1], w2[1])
-        for g in range(1, PASSES):
+        for g in range(W1_TILES - PASSES):
             load_w1(1, g)
 
         nc.gpsimd.memset(windows[0][:], 0.0)
         nc.scalar.activation(windows[1][:], windows[0][:], ACT.Copy)
         nc.gpsimd.memset(windows[2][:], 0.0)
+        for tile in x_raw:
+            nc.gpsimd.memset(tile[:, PACK * T:(PACK - 1) * T + WIDE], 0.0)
 
         def slots(e, first=0, count=C):
             start = (e * C + first) // PER_COL
@@ -94,83 +104,113 @@ def tile_moe_pre_mlp_relu2_kernel(tc, xT, w1, w2, gate, offs, out):
             nc.vector.quantize_mx(out=codes[:].bitcast(FP8X4), scales=scales[:], in_=values[:, :])
             return codes, scales
 
-        def pairs(ap, order):
-            return ap.rearrange(f"p ({order}) -> p c j i", i=2, j=PACK)
+        def quads(ap, order):
+            return ap.rearrange(f"p ({order}) -> p c j i", i=4, j=PACK)
 
-        def gather(e, g, dst):
-            for j in range(PACK):
-                nc.scalar.activation(dst[:, j * C:(j + 1) * C], x_window(g, j).indirect(slots(e)), ACT.Copy)
-
-        def gate_and_weave(e, src, dst):
-            weight = gate_sb[:, e * C:(e + 1) * C].rearrange("p (c i) -> p c i", i=2)
+        def gate_and_weave(src, dst, first, count):
+            weight = gate_sb[:, first:first + count].rearrange("p (c i) -> p c i", i=4)
             nc.vector.tensor_tensor(
-                pairs(dst[:, 0:C * PACK], "c i j"),
-                pairs(src[:], "j c i"),
-                weight.unsqueeze(2).to_broadcast([P, C // 2, PACK, 2]),
+                quads(dst, "c i j"),
+                src,
+                weight.unsqueeze(2).to_broadcast([P, count // 4, PACK, 4]),
                 ALU.mult,
             )
 
-        def gather_gated(e, g, dst):
+        def gather(g):
+            dst = gathered[g % 2]
             for j in range(PACK):
-                nc.vector.tensor_tensor(
-                    gated[:, j * C:(j + 1) * C], x_window(g, j).indirect(slots(e)), gate_sb[:, e * C:(e + 1) * C], ALU.mult
-                )
-            nc.vector.tensor_copy(pairs(dst[:, 0:C * PACK], "c i j"), pairs(gated[:], "j c i"))
+                if g < SHARED:
+                    nc.scalar.activation(dst[:, j * C:(j + 1) * C], x_rows[g][j][:].indirect(slots(0)), ACT.Copy)
+                elif g < PLANES:
+                    nc.scalar.activation(dst[:, j * S:(j + 1) * S], x_rows[g][j][:].indirect(offsets[:]), ACT.Copy)
+                else:
+                    window = x_raw[g - PLANES][:, j * T:j * T + WIDE]
+                    nc.scalar.activation(dst[:, j * S:(j + 1) * S], window.indirect(offsets[:]), ACT.Copy)
+
+        def weave_x(e, g, dst):
+            if g < SHARED:
+                for j in range(PACK):
+                    nc.vector.tensor_tensor(
+                        gated[:, j * C:(j + 1) * C], x_rows[g][j][:].indirect(slots(1)), gate_sb[:, C:S], ALU.mult
+                    )
+                gate_and_weave(quads(gathered[g % 2][:, 0:PACK * C], "j c i"), dst[:, 0:PACK * C], 0, C)
+                nc.vector.tensor_copy(quads(dst[:, PACK * C:PACK * S], "c i j"), quads(gated[:], "j c i"))
+            elif g < PASSES - 1:
+                gate_and_weave(quads(gathered[g % 2][:], "j c i"), dst[:], 0, S)
+            else:
+                src = quads(gathered[g % 2][:], "j c i")[:, e * C // 4:(e + 1) * C // 4]
+                gate_and_weave(src, dst[:, 0:PACK * C], e * C, C)
+            if g + 2 < PASSES:
+                gather(g + 2)
 
         def weave_w1(e, g, dst, split):
             to = dst[:].rearrange("p (u i m j) -> p u m j i", u=2, i=2, j=PACK)
             fro = w1_raw[e][g][:].rearrange("p (j m u i) -> p u m j i", u=2, i=2, j=PACK)
-            if split > 0:
+            if (e, g) == (E - 1, PASSES - 1):
+                for u in range(2):
+                    nc.vector.tensor_copy(to[:, u], fro[:, u])
+            elif split > 0:
                 nc.vector.tensor_copy(to[:, :, 0:split], fro[:, :, 0:split])
             if split < P:
                 nc.scalar.copy(to[:, :, split:P], fro[:, :, split:P])
 
-        def second_weights(e):
-            nc.scalar.copy(pairs(w2_bf[:], "c i j"), pairs(w2_raw[e][:], "j c i"))
+        def second_weights(e, split):
+            to = quads(w2_bf[:], "c i j")
+            fro = quads(w2_raw[e][:], "j c i")
+            if split > 0:
+                nc.vector.tensor_copy(to[:, 0:split], fro[:, 0:split])
+            nc.scalar.copy(to[:, split:N // 4], fro[:, split:N // 4])
+            return quantize(w2_bf, N, f"w2{e}")
 
-        def first_product(banks, g, w_q, x_q):
+        def first_product(e, g, w_q, first, tiles):
             for half in range(2):
-                for t in range(PACK):
+                for t in tiles:
+                    cols = slice((t - first) * P, (t - first + 1) * P)
+                    base = e * C if g < PASSES - 1 else 0
+                    picked = slice(base + half * HALF, base + (half + 1) * HALF)
                     nc.tensor.matmul_mx(
-                        out=banks[half][:, t * HALF:(t + 1) * HALF],
-                        lhsT=w_q[0][:, t * P:(t + 1) * P].bitcast(FP8X4),
-                        lhsT_scale=w_q[1][:, t * P:(t + 1) * P],
-                        rhs=x_q[0][:, half * HALF:(half + 1) * HALF].bitcast(FP8X4),
-                        rhs_scale=x_q[1][:, half * HALF:(half + 1) * HALF],
+                        out=a_banks[e][half][:, t * HALF:(t + 1) * HALF],
+                        lhsT=w_q[0][:, cols].bitcast(FP8X4),
+                        lhsT_scale=w_q[1][:, cols],
+                        rhs=x_q[e, g][0][:, picked].bitcast(FP8X4),
+                        rhs_scale=x_q[e, g][1][:, picked],
                         start=(g == 0 and t == 0),
                         stop=(g == PASSES - 1 and t == PACK - 1),
                     )
 
-        def hidden(bank, on_scalar, name):
-            positive = ring.tile([P, HALF * PACK], F32, name="positive")
-            h_bf = ring.tile([P, HALF * PACK], BF16, name="h_bf", align_bytes=64)
-            src = bank[:].rearrange("p (t c) -> p c t", t=PACK)
-            dst = positive[:].rearrange("p (c t) -> p c t", t=PACK)
-            if on_scalar:
-                nc.scalar.activation(dst, src, ACT.Relu)
-                nc.scalar.activation(h_bf[:], positive[:], ACT.Square)
-            else:
-                nc.vector.tensor_scalar(dst, src, 0.0, None, ALU.max)
-                nc.vector.tensor_tensor(h_bf[:], positive[:], positive[:], ALU.mult)
-            return quantize(h_bf, HALF, name)
+        def hidden(e, on_scalar):
+            codes = keep.tile([P, C], U32, name=f"h{e}_codes", align_bytes=64)
+            scales = keep.tile([P, C], U8, name=f"h{e}_scales", align_bytes=64)
+            for half in range(2):
+                positive = ring.tile([P, HALF * PACK], F32, name="positive")
+                h_bf = ring.tile([P, HALF * PACK], BF16, name="h_bf", align_bytes=64)
+                src = a_banks[e][half][:].rearrange("p (t c) -> p c t", t=PACK)
+                dst = positive[:].rearrange("p (c t) -> p c t", t=PACK)
+                if on_scalar[half]:
+                    nc.scalar.activation(dst, src, ACT.Relu)
+                    nc.scalar.activation(h_bf[:], positive[:], ACT.Square)
+                else:
+                    nc.vector.tensor_scalar(dst, src, 0.0, None, ALU.max)
+                    nc.vector.tensor_tensor(h_bf[:], positive[:], positive[:], ALU.mult)
+                cols = slice(half * HALF, (half + 1) * HALF)
+                nc.vector.quantize_mx(out=codes[:, cols].bitcast(FP8X4), scales=scales[:, cols], in_=h_bf[:])
+            return codes, scales
 
-        def second_product(bank, w_q, h_q, y, half, on_scalar):
-            for b in range(N_BLOCKS):
-                nc.tensor.matmul_mx(
-                    out=bank[:, b * HALF:(b + 1) * HALF],
-                    lhsT=w_q[0][:, b * P:(b + 1) * P].bitcast(FP8X4),
-                    lhsT_scale=w_q[1][:, b * P:(b + 1) * P],
-                    rhs=h_q[0][:].bitcast(FP8X4),
-                    rhs_scale=h_q[1][:],
-                    start=True,
-                    stop=True,
-                )
-            dst = y[:].rearrange("p (b c) -> p b c", b=N_BLOCKS)[:, :, half * HALF:(half + 1) * HALF]
-            src = bank[:].rearrange("p (b c) -> p b c", b=N_BLOCKS)
+        def second_product(e, b, w_q, h_q, on_scalar):
+            bank = psum.tile([P, C], F32, name=f"y_bank{b}")
+            nc.tensor.matmul_mx(
+                out=bank[:],
+                lhsT=w_q[0][:, b * P:(b + 1) * P].bitcast(FP8X4),
+                lhsT_scale=w_q[1][:, b * P:(b + 1) * P],
+                rhs=h_q[0][:].bitcast(FP8X4),
+                rhs_scale=h_q[1][:],
+                start=True,
+                stop=True,
+            )
             if on_scalar:
-                nc.scalar.copy(dst, src)
+                nc.scalar.copy(ys[e][:, b * C:(b + 1) * C], bank[:])
             else:
-                nc.vector.tensor_copy(dst, src)
+                nc.vector.tensor_copy(ys[e][:, b * C:(b + 1) * C], bank[:])
 
         def scatter(y, e, b, first, count, on_scalar):
             target = windows[b][:].indirect(slots(e, first, count))
@@ -181,62 +221,67 @@ def tile_moe_pre_mlp_relu2_kernel(tc, xT, w1, w2, gate, offs, out):
                 nc.vector.tensor_copy(target, values)
 
         a_banks = [[psum.tile([P, PACK * HALF], F32, name=f"a{e}_{h}") for h in range(2)] for e in range(E)]
-        y_banks = [[psum.tile([P, N_BLOCKS * HALF], F32, name=f"yb{e}_{h}") for h in range(2)] for e in range(E)]
         ys = [keep.tile([P, N_BLOCKS * C], F32, name=f"y{e}") for e in range(E)]
 
         x_q = {}
-        w2_q = {}
-        h_q = {}
-        on_scalar = [(e, g) for g in range(PASSES) for e in range(E) if not (g < SHARED and e == 1)]
-        for i in range(2):
-            gather(on_scalar[i][0], on_scalar[i][1], gathered[i])
+        gather(0)
+        gather(1)
 
-        def finish(step, i):
+        def finish(step, src):
             kind, e, g = step
-            if kind == "x":
-                x_q[e, g] = quantize(stage[i % 2][:, 0:C * PACK], C, f"x{e}_{g}")
+            if kind == "x" and g < PASSES - 1:
+                x_q[0, g] = quantize(src, S, f"x{g}")
+                x_q[1, g] = x_q[0, g]
+            elif kind == "x":
+                x_q[e, g] = quantize(src[:, 0:PACK * C], C, f"x{g}_{e}")
+            elif (e, g) != (E - 1, PASSES - 1):
+                first_product(e, g, quantize(src, H, "w1", ring), 0, range(PACK))
             else:
-                first_product(a_banks[e], g, quantize(stage[i % 2], H, "w1", ring), x_q[e, g])
+                for t in range(0, PACK, 2):
+                    part = quantize(src[:, t * K_PASS:(t + 2) * K_PASS], 2 * P, f"w1_last{t}")
+                    first_product(e, g, part, t, range(t, t + 2))
 
-        def expert_zero_hidden():
-            second_weights(0)
-            w2_q[0] = quantize(w2_bf, N, "w20")
-            for h in range(2):
-                h_q[0, h] = hidden(a_banks[0][h], True, f"h0_{h}")
-            for h in range(2):
-                second_product(y_banks[0][h], w2_q[0], h_q[0, h], ys[0], h, True)
-            second_weights(1)
-            w2_q[1] = quantize(w2_bf, N, "w21")
+        def expert_zero_rest():
+            w2_q = second_weights(0, 0)
+            h_q = hidden(0, H0S)
+            for b in range(N_BLOCKS):
+                second_product(0, b, w2_q, h_q, True)
             for b in range(N_BLOCKS):
                 scatter(ys[0], 0, b, 0, C, True)
 
-        steps = [("x", 1, 0), ("x", 0, 0), ("x", 1, 1), ("x", 0, 1), ("w", 0, 0), ("x", 0, 2), ("x", 1, 2), ("w", 0, 1),
-                 ("x", 0, 3), ("x", 1, 3), ("w", 0, 2), ("x", 0, 4), ("w", 0, 3), ("w", 0, 4), ("x", 1, 4),
-                 ("w", 1, 0), ("w", 1, 1), ("w", 1, 2), ("w", 1, 3), ("w", 1, 4)]
-        for i, step in enumerate(steps):
+        steps = STEPS
+        waiting = []
+        turn = 0
+        for step in steps:
             kind, e, g = step
-            dst = stage[i % 2]
-            if kind == "w":
-                weave_w1(e, g, dst, {(0, 4): 0, (1, 4): 88}.get((e, g), P))
-            elif (e, g) in on_scalar:
-                n = on_scalar.index((e, g))
-                gate_and_weave(e, gathered[n % 3], dst)
-                if n + 2 < len(on_scalar):
-                    gather(on_scalar[n + 2][0], on_scalar[n + 2][1], gathered[(n + 2) % 3])
+            if kind == "w" and (e, g) in ON_S:
+                dst = side[ON_S[e, g]]
+                weave_w1(e, g, dst, 0)
             else:
-                gather_gated(e, g, dst)
-            if i > 0:
-                finish(steps[i - 1], i - 1)
-            if step == ("w", 1, 0):
-                expert_zero_hidden()
-        finish(steps[-1], len(steps) - 1)
+                dst = stage[turn % 2]
+                turn = turn + 1
+                if kind == "w":
+                    weave_w1(e, g, dst, LAST if (e, g) == (1, 4) else P)
+                else:
+                    weave_x(e, g, dst)
+            if step == ("w", 0, 1):
+                for late in range(W1_TILES - PASSES, PASSES):
+                    load_w1(1, late)
+                load_rows(w2_raw[1], w2[1])
+            for before, src in waiting:
+                finish(before, src)
+            if waiting and waiting[0][0] == ("w", 0, 4):
+                expert_zero_rest()
+            waiting = [(step, dst)]
+        finish(waiting[0][0], waiting[0][1])
 
-        for h in range(2):
-            h_q[1, h] = hidden(a_banks[1][h], h == 0, f"h1_{h}")
-        for h in range(2):
-            second_product(y_banks[1][h], w2_q[1], h_q[1, h], ys[1], h, h == 0)
-        scatter(ys[1], 1, 2, 0, HALF, True)
+        w2_q = second_weights(1, W2L)
+        h_q = hidden(1, [False, True])
+        second_product(1, 0, w2_q, h_q, False)
+        second_product(1, 2, w2_q, h_q, True)
+        second_product(1, 1, w2_q, h_q, True)
         scatter(ys[1], 1, 0, 0, C, False)
+        scatter(ys[1], 1, 2, 0, HALF, True)
         scatter(ys[1], 1, 1, 0, C, True)
         scatter(ys[1], 1, 2, HALF, HALF, False)
         for b in range(N_BLOCKS):

@@ -1,6 +1,7 @@
 from contextlib import ExitStack
 
 import concourse.mybir as mybir
+from concourse.masks import make_identity
 
 K, T, E, C, H, N = 2560, 640, 2, 256, 512, 384
 FLOPS = 2 * E * C * (K * H + H * N)
@@ -27,7 +28,10 @@ PLANES = 3
 LOADS = [("x", 3), ("w", 0), ("x", 4), ("w", 1), ("w", 2), ("w", 3), ("w", 4)]
 LEAD = 1
 W1_TILES = 8
-ON_S = {(0, 3): 0, (0, 4): 1}
+SPLITQ0 = False
+SIDES = 3
+SUB = 1
+ON_S = [(0, 2, 1), (0, 3, 0), (0, 3, 1), (0, 4, 0), (0, 4, 1), (1, 1, 1)]
 H0S = [True, True]
 Y0S = [True, True]
 SC0V = 0
@@ -56,7 +60,7 @@ def tile_moe_pre_mlp_relu2_kernel(tc, xT, w1, w2, gate, offs, out):
         gathered = [keep.tile([P, PACK * S], F32, name=f"gathered{i}") for i in range(2)]
         gated = keep.tile([P, PACK * C], F32, name="gated")
         stage = [keep.tile([P, PACK * H], BF16, name=f"stage{i}", align_bytes=64) for i in range(2)]
-        side = [keep.tile([P, PACK * H], BF16, name=f"side{i}", align_bytes=64) for i in range(2)]
+        side = [keep.tile([P, PACK * H], BF16, name=f"side{i}", align_bytes=64) for i in range(SIDES)]
         w2_bf = keep.tile([P, PACK * N], BF16, name="w2_bf", align_bytes=64)
 
         def load_rows(dst, rows):
@@ -72,13 +76,12 @@ def tile_moe_pre_mlp_relu2_kernel(tc, xT, w1, w2, gate, offs, out):
         def load_w1(e, g):
             load_rows(w1_raw[e][g], w1[e, g * K_PASS:(g + 1) * K_PASS, :])
 
+        gate_cols = keep.tile([P, S // P], F32, name="gate_cols")
+        nc.sync.dma_start(out=gate_cols[:], in_=gate[0:1, :].rearrange("o (p m) -> (o p) m", p=P))
         nc.sync.dma_start(offsets[:], offs)
-        load_x_row(0, 0)
-        nc.sync.dma_start(out=gate_sb[:], in_=gate[0:P, :])
         for g in range(PLANES):
             for j in range(PACK):
-                if g + j > 0:
-                    load_x_row(g, j)
+                load_x_row(g, j)
         for kind, g in LOADS:
             if kind == "x":
                 load_x(g)
@@ -88,7 +91,15 @@ def tile_moe_pre_mlp_relu2_kernel(tc, xT, w1, w2, gate, offs, out):
         for g in range(W1_TILES - PASSES):
             load_w1(1, g)
 
+        identity = keep.tile([P, P], F32, name="identity")
         nc.gpsimd.memset(windows[0][:], 0.0)
+        make_identity(nc, identity[:])
+        gate_bank = psum.tile([P, S], F32, name="gate_bank")
+        for m in range(S // P):
+            nc.tensor.transpose(gate_bank[:, m * P:(m + 1) * P], gate_cols[:, m:m + 1].to_broadcast([P, P]), identity[:])
+        nc.vector.tensor_copy(
+            gate_sb[:].rearrange("p (n m) -> p n m", m=S // P), gate_bank[:].rearrange("p (m n) -> p n m", m=S // P)
+        )
         nc.scalar.activation(windows[1][:], windows[0][:], ACT.Copy)
         nc.gpsimd.memset(windows[2][:], 0.0)
         for tile in x_raw:
@@ -143,16 +154,14 @@ def tile_moe_pre_mlp_relu2_kernel(tc, xT, w1, w2, gate, offs, out):
             if g + 2 < PASSES:
                 gather(g + 2)
 
-        def weave_w1(e, g, dst, split):
+        def weave_w1(e, g, dst):
             to = dst[:].rearrange("p (u i m j) -> p u m j i", u=2, i=2, j=PACK)
             fro = w1_raw[e][g][:].rearrange("p (j m u i) -> p u m j i", u=2, i=2, j=PACK)
-            if (e, g) == (E - 1, PASSES - 1):
-                for u in range(2):
+            for u in range(2):
+                if (e, g, u) in ON_S:
+                    nc.scalar.copy(to[:, u], fro[:, u])
+                else:
                     nc.vector.tensor_copy(to[:, u], fro[:, u])
-            elif split > 0:
-                nc.vector.tensor_copy(to[:, :, 0:split], fro[:, :, 0:split])
-            if split < P:
-                nc.scalar.copy(to[:, :, split:P], fro[:, :, split:P])
 
         def second_weights(e, split):
             to = quads(w2_bf[:], "c i j")
@@ -186,12 +195,20 @@ def tile_moe_pre_mlp_relu2_kernel(tc, xT, w1, w2, gate, offs, out):
                 h_bf = ring.tile([P, HALF * PACK], BF16, name="h_bf", align_bytes=64)
                 src = a_banks[e][half][:].rearrange("p (t c) -> p c t", t=PACK)
                 dst = positive[:].rearrange("p (c t) -> p c t", t=PACK)
-                if on_scalar[half]:
-                    nc.scalar.activation(dst, src, ACT.Relu)
-                    nc.scalar.activation(h_bf[:], positive[:], ACT.Square)
-                else:
-                    nc.vector.tensor_scalar(dst, src, 0.0, None, ALU.max)
-                    nc.vector.tensor_tensor(h_bf[:], positive[:], positive[:], ALU.mult)
+                parts = SUB if e == 1 else 1
+                width = HALF // parts
+                for k in range(parts):
+                    part = slice(k * width, (k + 1) * width)
+                    if on_scalar[half]:
+                        nc.scalar.activation(dst[:, part], src[:, part], ACT.Relu)
+                    else:
+                        nc.vector.tensor_scalar(dst[:, part], src[:, part], 0.0, None, ALU.max)
+                for k in range(parts):
+                    part = slice(k * width * PACK, (k + 1) * width * PACK)
+                    if on_scalar[half]:
+                        nc.scalar.activation(h_bf[:, part], positive[:, part], ACT.Square)
+                    else:
+                        nc.vector.tensor_tensor(h_bf[:, part], positive[:, part], positive[:, part], ALU.mult)
                 cols = slice(half * HALF, (half + 1) * HALF)
                 nc.vector.quantize_mx(out=codes[:, cols].bitcast(FP8X4), scales=scales[:, cols], in_=h_bf[:])
             return codes, scales
@@ -234,11 +251,11 @@ def tile_moe_pre_mlp_relu2_kernel(tc, xT, w1, w2, gate, offs, out):
                 x_q[1, g] = x_q[0, g]
             elif kind == "x":
                 x_q[e, g] = quantize(src[:, 0:PACK * C], C, f"x{g}_{e}")
-            elif (e, g) != (E - 1, PASSES - 1):
+            elif e == 0 and not SPLITQ0:
                 first_product(e, g, quantize(src, H, "w1", ring), 0, range(PACK))
             else:
                 for t in range(0, PACK, 2):
-                    part = quantize(src[:, t * K_PASS:(t + 2) * K_PASS], 2 * P, f"w1_last{t}")
+                    part = quantize(src[:, t * K_PASS:(t + 2) * K_PASS], 2 * P, f"w1_half{t}", ring)
                     first_product(e, g, part, t, range(t, t + 2))
 
         def expert_zero_rest():
@@ -252,18 +269,19 @@ def tile_moe_pre_mlp_relu2_kernel(tc, xT, w1, w2, gate, offs, out):
         steps = STEPS
         waiting = []
         turn = 0
+        aside = 0
         for step in steps:
             kind, e, g = step
-            if kind == "w" and (e, g) in ON_S:
-                dst = side[ON_S[e, g]]
-                weave_w1(e, g, dst, 0)
+            if kind == "w" and ((e, g, 0) in ON_S or (e, g, 1) in ON_S):
+                dst = side[aside % SIDES]
+                aside = aside + 1
             else:
                 dst = stage[turn % 2]
                 turn = turn + 1
-                if kind == "w":
-                    weave_w1(e, g, dst, LAST if (e, g) == (1, 4) else P)
-                else:
-                    weave_x(e, g, dst)
+            if kind == "w":
+                weave_w1(e, g, dst)
+            else:
+                weave_x(e, g, dst)
             if step == ("w", 0, 1):
                 for late in range(W1_TILES - PASSES, PASSES):
                     load_w1(1, late)

@@ -4,8 +4,9 @@ import concourse.mybir as mybir
 from concourse.masks import make_identity
 
 K, T, E, C, H, N = 2560, 640, 2, 256, 512, 384
-FLOPS = 2 * E * C * (K * H + H * N)
-BYTES = 4 * (K * T + E * K * H + E * H * N + E * C + N * T) + 2 * 128 * (E * C // 16)
+SLOTS = E * C
+FLOPS = 2 * SLOTS * (K * H + H * N)
+BYTES = 4 * (K * T + E * K * H + E * H * N + SLOTS + N * T) + 2 * 128 * (SLOTS // 16)
 
 F32 = mybir.dt.float32
 BF16 = mybir.dt.bfloat16
@@ -20,26 +21,19 @@ P = 128
 PACK = 4
 K_PASS = P * PACK
 PASSES = K // K_PASS
+LAST = PASSES - 1
 HALF = C // 2
 N_BLOCKS = N // P
-PER_COL = 16
-SHARED = 2
-PLANES = 3
-LOADS = [("x", 3), ("w", 0), ("x", 4), ("w", 1), ("w", 2), ("w", 3), ("w", 4)]
-LEAD = 1
+PER_COLUMN = 16
+LINE = 4
+
+FUSED_PASSES = 2
+ROW_PASSES = 3
+WINDOW = 2 * SLOTS
 W1_TILES = 8
-SPLITQ0 = False
-SIDES = 3
-SUB = 1
-ON_S = [(0, 2, 1), (0, 3, 0), (0, 3, 1), (0, 4, 0), (0, 4, 1), (1, 1, 1)]
-H0S = [True, True]
-Y0S = [True, True]
-SC0V = 0
-LAST = 128
-W2L = 32
-STEPS = [("x", 0, 0), ("x", 0, 1), ("x", 0, 2), ("w", 0, 0), ("x", 0, 3), ("w", 0, 1), ("x", 0, 4), ("w", 0, 2), ("x", 1, 4), ("w", 0, 3), ("w", 0, 4), ("w", 1, 0), ("w", 1, 1), ("w", 1, 2), ("w", 1, 3), ("w", 1, 4)]
-S = E * C
-WIDE = 2 * S
+SCALAR_FROM_HALF = 5
+SCALAR_PASS_OF_EXPERT_1 = 1
+W2_GROUPS_ON_VECTOR = 48
 
 
 def tile_moe_pre_mlp_relu2_kernel(tc, xT, w1, w2, gate, offs, out):
@@ -49,258 +43,270 @@ def tile_moe_pre_mlp_relu2_kernel(tc, xT, w1, w2, gate, offs, out):
         ring = ctx.enter_context(tc.tile_pool(name="ring", bufs=3))
         psum = ctx.enter_context(tc.psum_pool(name="psum", bufs=1))
 
-        offsets = keep.tile([P, E * C // PER_COL], U16, name="offsets")
-        gate_sb = keep.tile([P, E * C], F32, name="gate_sb")
-        x_rows = [[keep.tile([P, T], F32, name=f"x_row{g}_{j}") for j in range(PACK)] for g in range(PLANES)]
-        x_raw = [keep.tile([P, (PACK - 1) * T + WIDE], F32, name=f"x_raw{g}") for g in range(PLANES, PASSES)]
+        offsets = keep.tile([P, SLOTS // PER_COLUMN], U16, name="offsets")
+        gate_sb = keep.tile([P, SLOTS], F32, name="gate_sb")
+        x_rows = [[keep.tile([P, T], F32, name=f"x_row{g}_{j}") for j in range(PACK)] for g in range(ROW_PASSES)]
+        x_passes = {g: keep.tile([P, (PACK - 1) * T + WINDOW], F32, name=f"x_pass{g}") for g in range(ROW_PASSES, PASSES)}
         w1_tiles = [keep.tile([P, PACK * H], F32, name=f"w1_raw{i}") for i in range(W1_TILES)]
-        w1_raw = [[w1_tiles[(e * PASSES + g) % W1_TILES] for g in range(PASSES)] for e in range(E)]
         w2_raw = [keep.tile([P, PACK * N], F32, name=f"w2_raw{e}") for e in range(E)]
-        windows = [keep.tile([P, T], F32, name=f"window{b}") for b in range(N_BLOCKS)]
-        gathered = [keep.tile([P, PACK * S], F32, name=f"gathered{i}") for i in range(2)]
+        out_sb = [keep.tile([P, T], F32, name=f"out_sb{b}") for b in range(N_BLOCKS)]
+        gathered = [keep.tile([P, PACK * SLOTS], F32, name=f"gathered{i}") for i in range(2)]
         gated = keep.tile([P, PACK * C], F32, name="gated")
-        stage = [keep.tile([P, PACK * H], BF16, name=f"stage{i}", align_bytes=64) for i in range(2)]
-        side = [keep.tile([P, PACK * H], BF16, name=f"side{i}", align_bytes=64) for i in range(SIDES)]
-        w2_bf = keep.tile([P, PACK * N], BF16, name="w2_bf", align_bytes=64)
+        woven_vector = [keep.tile([P, PACK * H], BF16, name=f"woven_vector{i}", align_bytes=64) for i in range(2)]
+        woven_shared = [keep.tile([P, PACK * H], BF16, name=f"woven_shared{i}", align_bytes=64) for i in range(3)]
+        woven_w2 = keep.tile([P, PACK * N], BF16, name="woven_w2", align_bytes=64)
 
-        def load_rows(dst, rows):
-            nc.sync.dma_start(out=dst[:, :], in_=rows.rearrange("(p j) w -> p (j w)", j=PACK))
+        def w1_raw(e, g):
+            return w1_tiles[(e * PASSES + g) % W1_TILES]
+
+        def load_pass(dst, rows):
+            nc.sync.dma_start(out=dst, in_=rows.rearrange("(p j) w -> p (j w)", j=PACK))
 
         def load_x_row(g, j):
             rows = xT[g * K_PASS:(g + 1) * K_PASS, :].rearrange("(p j) w -> p j w", j=PACK)
             nc.sync.dma_start(out=x_rows[g][j][:], in_=rows[:, j, :])
 
-        def load_x(g):
-            load_rows(x_raw[g - PLANES][:, 0:PACK * T], xT[g * K_PASS:(g + 1) * K_PASS, :])
-
         def load_w1(e, g):
-            load_rows(w1_raw[e][g], w1[e, g * K_PASS:(g + 1) * K_PASS, :])
+            load_pass(w1_raw(e, g)[:], w1[e, g * K_PASS:(g + 1) * K_PASS, :])
 
-        gate_cols = keep.tile([P, S // P], F32, name="gate_cols")
-        nc.sync.dma_start(out=gate_cols[:], in_=gate[0:1, :].rearrange("o (p m) -> (o p) m", p=P))
-        nc.sync.dma_start(offsets[:], offs)
-        for g in range(PLANES):
+        per_partition = SLOTS // P
+        gate_cols = keep.tile([P, per_partition], F32, name="gate_cols")
+        nc.scalar.dma_start(out=gate_cols[:], in_=gate[0:1, :].rearrange("o (n m) -> (o n) m", n=P))
+        for g in range(ROW_PASSES):
             for j in range(PACK):
                 load_x_row(g, j)
-        for kind, g in LOADS:
-            if kind == "x":
-                load_x(g)
-            else:
-                load_w1(0, g)
-        load_rows(w2_raw[0], w2[0])
+                if (g, j) == (0, 0):
+                    nc.sync.dma_start(offsets[:], offs)
+        for g in range(PASSES):
+            if ROW_PASSES + g < PASSES:
+                x_pass = ROW_PASSES + g
+                load_pass(x_passes[x_pass][:, 0:PACK * T], xT[x_pass * K_PASS:(x_pass + 1) * K_PASS, :])
+            load_w1(0, g)
+        load_pass(w2_raw[0][:], w2[0])
         for g in range(W1_TILES - PASSES):
             load_w1(1, g)
 
         identity = keep.tile([P, P], F32, name="identity")
-        nc.gpsimd.memset(windows[0][:], 0.0)
+        nc.gpsimd.memset(out_sb[0][:], 0.0)
         make_identity(nc, identity[:])
-        gate_bank = psum.tile([P, S], F32, name="gate_bank")
-        for m in range(S // P):
+        gate_bank = psum.tile([P, SLOTS], F32, name="gate_bank")
+        for m in range(per_partition):
             nc.tensor.transpose(gate_bank[:, m * P:(m + 1) * P], gate_cols[:, m:m + 1].to_broadcast([P, P]), identity[:])
         nc.vector.tensor_copy(
-            gate_sb[:].rearrange("p (n m) -> p n m", m=S // P), gate_bank[:].rearrange("p (m n) -> p n m", m=S // P)
+            gate_sb[:].rearrange("p (n m) -> p n m", m=per_partition),
+            gate_bank[:].rearrange("p (m n) -> p n m", m=per_partition),
         )
-        nc.scalar.activation(windows[1][:], windows[0][:], ACT.Copy)
-        nc.gpsimd.memset(windows[2][:], 0.0)
-        for tile in x_raw:
-            nc.gpsimd.memset(tile[:, PACK * T:(PACK - 1) * T + WIDE], 0.0)
+        nc.scalar.activation(out_sb[2][:], out_sb[0][:], ACT.Copy)
+        nc.gpsimd.memset(out_sb[1][:], 0.0)
+        for g in range(ROW_PASSES, PASSES):
+            nc.gpsimd.memset(x_passes[g][:, PACK * T:(PACK - 1) * T + WINDOW], 0.0)
 
         def slots(e, first=0, count=C):
-            start = (e * C + first) // PER_COL
-            return offsets[:, start:start + count // PER_COL]
+            start = (e * C + first) // PER_COLUMN
+            return offsets[:, start:start + count // PER_COLUMN]
 
         def quantize(values, width, name, pool=keep):
             codes = pool.tile([P, width], U32, name=f"{name}_codes", align_bytes=64)
             scales = pool.tile([P, width], U8, name=f"{name}_scales", align_bytes=64)
-            nc.vector.quantize_mx(out=codes[:].bitcast(FP8X4), scales=scales[:], in_=values[:, :])
+            nc.vector.quantize_mx(out=codes[:].bitcast(FP8X4), scales=scales[:], in_=values)
             return codes, scales
 
-        def quads(ap, order):
-            return ap.rearrange(f"p ({order}) -> p c j i", i=4, j=PACK)
+        def by_lines(ap, order):
+            return ap.rearrange(f"p ({order}) -> p c j i", i=LINE, j=PACK)
 
         def gate_and_weave(src, dst, first, count):
-            weight = gate_sb[:, first:first + count].rearrange("p (c i) -> p c i", i=4)
+            weight = gate_sb[:, first:first + count].rearrange("p (c i) -> p c i", i=LINE)
             nc.vector.tensor_tensor(
-                quads(dst, "c i j"),
+                by_lines(dst, "c i j"),
                 src,
-                weight.unsqueeze(2).to_broadcast([P, count // 4, PACK, 4]),
+                weight.unsqueeze(2).to_broadcast([P, count // LINE, PACK, LINE]),
                 ALU.mult,
             )
 
-        def gather(g):
+        def gather_on_scalar(g):
             dst = gathered[g % 2]
             for j in range(PACK):
-                if g < SHARED:
+                if g < FUSED_PASSES:
                     nc.scalar.activation(dst[:, j * C:(j + 1) * C], x_rows[g][j][:].indirect(slots(0)), ACT.Copy)
-                elif g < PLANES:
-                    nc.scalar.activation(dst[:, j * S:(j + 1) * S], x_rows[g][j][:].indirect(offsets[:]), ACT.Copy)
                 else:
-                    window = x_raw[g - PLANES][:, j * T:j * T + WIDE]
-                    nc.scalar.activation(dst[:, j * S:(j + 1) * S], window.indirect(offsets[:]), ACT.Copy)
+                    window = x_rows[g][j][:] if g < ROW_PASSES else x_passes[g][:, j * T:j * T + WINDOW]
+                    nc.scalar.activation(dst[:, j * SLOTS:(j + 1) * SLOTS], window.indirect(offsets[:]), ACT.Copy)
 
         def weave_x(e, g, dst):
-            if g < SHARED:
+            src = gathered[g % 2]
+            if g < FUSED_PASSES:
                 for j in range(PACK):
                     nc.vector.tensor_tensor(
-                        gated[:, j * C:(j + 1) * C], x_rows[g][j][:].indirect(slots(1)), gate_sb[:, C:S], ALU.mult
+                        gated[:, j * C:(j + 1) * C], x_rows[g][j][:].indirect(slots(1)), gate_sb[:, C:SLOTS], ALU.mult
                     )
-                gate_and_weave(quads(gathered[g % 2][:, 0:PACK * C], "j c i"), dst[:, 0:PACK * C], 0, C)
-                nc.vector.tensor_copy(quads(dst[:, PACK * C:PACK * S], "c i j"), quads(gated[:], "j c i"))
-            elif g < PASSES - 1:
-                gate_and_weave(quads(gathered[g % 2][:], "j c i"), dst[:], 0, S)
+                gate_and_weave(by_lines(src[:, 0:PACK * C], "j c i"), dst[:, 0:PACK * C], 0, C)
+                nc.vector.tensor_copy(by_lines(dst[:, PACK * C:PACK * SLOTS], "c i j"), by_lines(gated[:], "j c i"))
+            elif g < LAST:
+                gate_and_weave(by_lines(src[:], "j c i"), dst[:], 0, SLOTS)
             else:
-                src = quads(gathered[g % 2][:], "j c i")[:, e * C // 4:(e + 1) * C // 4]
-                gate_and_weave(src, dst[:, 0:PACK * C], e * C, C)
+                groups = slice(e * C // LINE, (e + 1) * C // LINE)
+                gate_and_weave(by_lines(src[:], "j c i")[:, groups], dst[:, 0:PACK * C], e * C, C)
             if g + 2 < PASSES:
-                gather(g + 2)
+                gather_on_scalar(g + 2)
+
+        def w1_half_on_scalar(e, g, u):
+            if e == 0:
+                return 2 * g + u >= SCALAR_FROM_HALF
+            return g == SCALAR_PASS_OF_EXPERT_1 and u == 1
 
         def weave_w1(e, g, dst):
             to = dst[:].rearrange("p (u i m j) -> p u m j i", u=2, i=2, j=PACK)
-            fro = w1_raw[e][g][:].rearrange("p (j m u i) -> p u m j i", u=2, i=2, j=PACK)
+            fro = w1_raw(e, g)[:].rearrange("p (j m u i) -> p u m j i", u=2, i=2, j=PACK)
             for u in range(2):
-                if (e, g, u) in ON_S:
+                if w1_half_on_scalar(e, g, u):
                     nc.scalar.copy(to[:, u], fro[:, u])
                 else:
                     nc.vector.tensor_copy(to[:, u], fro[:, u])
 
-        def second_weights(e, split):
-            to = quads(w2_bf[:], "c i j")
-            fro = quads(w2_raw[e][:], "j c i")
-            if split > 0:
-                nc.vector.tensor_copy(to[:, 0:split], fro[:, 0:split])
-            nc.scalar.copy(to[:, split:N // 4], fro[:, split:N // 4])
-            return quantize(w2_bf, N, f"w2{e}")
+        woven_w2_lines = by_lines(woven_w2[:], "c i j")
 
-        def first_product(e, g, w_q, first, tiles):
+        def w2_lines(e):
+            return by_lines(w2_raw[e][:], "j c i")
+
+        a_banks = [[psum.tile([P, PACK * HALF], F32, name=f"a{e}_{half}") for half in range(2)] for e in range(E)]
+        y_sb = [keep.tile([P, N_BLOCKS * C], F32, name=f"y{e}") for e in range(E)]
+        x_q = {}
+
+        def first_product(e, g, w_q, tiles):
+            x_codes, x_scales, base = x_q[e, g]
             for half in range(2):
+                picked = slice(base + half * HALF, base + (half + 1) * HALF)
                 for t in tiles:
-                    cols = slice((t - first) * P, (t - first + 1) * P)
-                    base = e * C if g < PASSES - 1 else 0
-                    picked = slice(base + half * HALF, base + (half + 1) * HALF)
+                    cols = slice((t - tiles.start) * P, (t - tiles.start + 1) * P)
                     nc.tensor.matmul_mx(
                         out=a_banks[e][half][:, t * HALF:(t + 1) * HALF],
                         lhsT=w_q[0][:, cols].bitcast(FP8X4),
                         lhsT_scale=w_q[1][:, cols],
-                        rhs=x_q[e, g][0][:, picked].bitcast(FP8X4),
-                        rhs_scale=x_q[e, g][1][:, picked],
+                        rhs=x_codes[:, picked].bitcast(FP8X4),
+                        rhs_scale=x_scales[:, picked],
                         start=(g == 0 and t == 0),
-                        stop=(g == PASSES - 1 and t == PACK - 1),
+                        stop=(g == LAST and t == PACK - 1),
                     )
 
-        def hidden(e, on_scalar):
+        def hidden(e, on_scalar, parts):
             codes = keep.tile([P, C], U32, name=f"h{e}_codes", align_bytes=64)
             scales = keep.tile([P, C], U8, name=f"h{e}_scales", align_bytes=64)
+            width = HALF // parts
             for half in range(2):
                 positive = ring.tile([P, HALF * PACK], F32, name="positive")
                 h_bf = ring.tile([P, HALF * PACK], BF16, name="h_bf", align_bytes=64)
                 src = a_banks[e][half][:].rearrange("p (t c) -> p c t", t=PACK)
                 dst = positive[:].rearrange("p (c t) -> p c t", t=PACK)
-                parts = SUB if e == 1 else 1
-                width = HALF // parts
-                for k in range(parts):
-                    part = slice(k * width, (k + 1) * width)
+                for part in range(parts):
+                    part_slots = slice(part * width, (part + 1) * width)
                     if on_scalar[half]:
-                        nc.scalar.activation(dst[:, part], src[:, part], ACT.Relu)
+                        nc.scalar.activation(dst[:, part_slots], src[:, part_slots], ACT.Relu)
                     else:
-                        nc.vector.tensor_scalar(dst[:, part], src[:, part], 0.0, None, ALU.max)
-                for k in range(parts):
-                    part = slice(k * width * PACK, (k + 1) * width * PACK)
+                        nc.vector.tensor_scalar(dst[:, part_slots], src[:, part_slots], 0.0, None, ALU.max)
+                for part in range(parts):
+                    values = slice(part * width * PACK, (part + 1) * width * PACK)
                     if on_scalar[half]:
-                        nc.scalar.activation(h_bf[:, part], positive[:, part], ACT.Square)
+                        nc.scalar.activation(h_bf[:, values], positive[:, values], ACT.Square)
                     else:
-                        nc.vector.tensor_tensor(h_bf[:, part], positive[:, part], positive[:, part], ALU.mult)
+                        nc.vector.tensor_tensor(h_bf[:, values], positive[:, values], positive[:, values], ALU.mult)
                 cols = slice(half * HALF, (half + 1) * HALF)
                 nc.vector.quantize_mx(out=codes[:, cols].bitcast(FP8X4), scales=scales[:, cols], in_=h_bf[:])
             return codes, scales
 
-        def second_product(e, b, w_q, h_q, on_scalar):
+        def second_product(e, b, w_codes, w_scales, h_q, on_scalar):
             bank = psum.tile([P, C], F32, name=f"y_bank{b}")
             nc.tensor.matmul_mx(
                 out=bank[:],
-                lhsT=w_q[0][:, b * P:(b + 1) * P].bitcast(FP8X4),
-                lhsT_scale=w_q[1][:, b * P:(b + 1) * P],
+                lhsT=w_codes.bitcast(FP8X4),
+                lhsT_scale=w_scales,
                 rhs=h_q[0][:].bitcast(FP8X4),
                 rhs_scale=h_q[1][:],
                 start=True,
                 stop=True,
             )
             if on_scalar:
-                nc.scalar.copy(ys[e][:, b * C:(b + 1) * C], bank[:])
+                nc.scalar.copy(y_sb[e][:, b * C:(b + 1) * C], bank[:])
             else:
-                nc.vector.tensor_copy(ys[e][:, b * C:(b + 1) * C], bank[:])
+                nc.vector.tensor_copy(y_sb[e][:, b * C:(b + 1) * C], bank[:])
 
-        def scatter(y, e, b, first, count, on_scalar):
-            target = windows[b][:].indirect(slots(e, first, count))
-            values = y[:, b * C + first:b * C + first + count]
+        def scatter(e, b, first, count, on_scalar):
+            target = out_sb[b][:].indirect(slots(e, first, count))
+            values = y_sb[e][:, b * C + first:b * C + first + count]
             if on_scalar:
                 nc.scalar.activation(target, values, ACT.Copy)
             else:
                 nc.vector.tensor_copy(target, values)
 
-        a_banks = [[psum.tile([P, PACK * HALF], F32, name=f"a{e}_{h}") for h in range(2)] for e in range(E)]
-        ys = [keep.tile([P, N_BLOCKS * C], F32, name=f"y{e}") for e in range(E)]
-
-        x_q = {}
-        gather(0)
-        gather(1)
-
-        def finish(step, src):
+        def quantize_step(step, src):
             kind, e, g = step
-            if kind == "x" and g < PASSES - 1:
-                x_q[0, g] = quantize(src, S, f"x{g}")
-                x_q[1, g] = x_q[0, g]
+            if kind == "x" and g < LAST:
+                codes, scales = quantize(src[:], SLOTS, f"x{g}")
+                for expert in range(E):
+                    x_q[expert, g] = (codes, scales, expert * C)
             elif kind == "x":
-                x_q[e, g] = quantize(src[:, 0:PACK * C], C, f"x{g}_{e}")
-            elif e == 0 and not SPLITQ0:
-                first_product(e, g, quantize(src, H, "w1", ring), 0, range(PACK))
+                codes, scales = quantize(src[:, 0:PACK * C], C, f"x{g}_{e}")
+                x_q[e, g] = (codes, scales, 0)
+            elif e == 0:
+                first_product(e, g, quantize(src[:], H, "w1", ring), range(PACK))
             else:
                 for t in range(0, PACK, 2):
-                    part = quantize(src[:, t * K_PASS:(t + 2) * K_PASS], 2 * P, f"w1_half{t}", ring)
-                    first_product(e, g, part, t, range(t, t + 2))
+                    w_q = quantize(src[:, t * K_PASS:(t + 2) * K_PASS], 2 * P, f"w1_half{t}", ring)
+                    first_product(e, g, w_q, range(t, t + 2))
 
-        def expert_zero_rest():
-            w2_q = second_weights(0, 0)
-            h_q = hidden(0, H0S)
-            for b in range(N_BLOCKS):
-                second_product(0, b, w2_q, h_q, True)
-            for b in range(N_BLOCKS):
-                scatter(ys[0], 0, b, 0, C, True)
+        later_x = [("x", 0, g) for g in range(ROW_PASSES, PASSES)] + [("x", 1, LAST)]
+        steps = [("x", 0, g) for g in range(ROW_PASSES)]
+        for g in range(PASSES):
+            steps.append(("w", 0, g))
+            steps.extend(later_x[g:g + 1])
+        steps.extend([("w", 1, g) for g in range(PASSES)])
 
-        steps = STEPS
-        waiting = []
-        turn = 0
-        aside = 0
+        gather_on_scalar(0)
+        gather_on_scalar(1)
+        vector_turn = 0
+        shared_turn = 0
+        before = None
         for step in steps:
             kind, e, g = step
-            if kind == "w" and ((e, g, 0) in ON_S or (e, g, 1) in ON_S):
-                dst = side[aside % SIDES]
-                aside = aside + 1
+            if kind == "w" and w1_half_on_scalar(e, g, 1):
+                dst = woven_shared[shared_turn % len(woven_shared)]
+                shared_turn = shared_turn + 1
             else:
-                dst = stage[turn % 2]
-                turn = turn + 1
+                dst = woven_vector[vector_turn % len(woven_vector)]
+                vector_turn = vector_turn + 1
             if kind == "w":
                 weave_w1(e, g, dst)
             else:
                 weave_x(e, g, dst)
-            if step == ("w", 0, 1):
+            if step == ("w", 0, E * PASSES - W1_TILES - 1):
                 for late in range(W1_TILES - PASSES, PASSES):
                     load_w1(1, late)
-                load_rows(w2_raw[1], w2[1])
-            for before, src in waiting:
-                finish(before, src)
-            if waiting and waiting[0][0] == ("w", 0, 4):
-                expert_zero_rest()
-            waiting = [(step, dst)]
-        finish(waiting[0][0], waiting[0][1])
+                load_pass(w2_raw[1][:], w2[1])
+            if before is not None:
+                quantize_step(before[0], before[1])
+            if step == ("w", 1, 0):
+                nc.scalar.copy(woven_w2_lines, w2_lines(0))
+                w2_q = quantize(woven_w2[:], N, "w2_0")
+                h_q = hidden(0, [True, True], 1)
+            if step == ("w", 1, SCALAR_PASS_OF_EXPERT_1):
+                for b in range(N_BLOCKS):
+                    cols = slice(b * P, (b + 1) * P)
+                    second_product(0, b, w2_q[0][:, cols], w2_q[1][:, cols], h_q, True)
+                for b in range(N_BLOCKS):
+                    scatter(0, b, 0, C, True)
+            before = (step, dst)
+        quantize_step(before[0], before[1])
 
-        w2_q = second_weights(1, W2L)
-        h_q = hidden(1, [False, True])
-        second_product(1, 0, w2_q, h_q, False)
-        second_product(1, 2, w2_q, h_q, True)
-        second_product(1, 1, w2_q, h_q, True)
-        scatter(ys[1], 1, 0, 0, C, False)
-        scatter(ys[1], 1, 2, 0, HALF, True)
-        scatter(ys[1], 1, 1, 0, C, True)
-        scatter(ys[1], 1, 2, HALF, HALF, False)
+        split = W2_GROUPS_ON_VECTOR
+        nc.vector.tensor_copy(woven_w2_lines[:, 0:split], w2_lines(1)[:, 0:split])
+        nc.scalar.copy(woven_w2_lines[:, split:N // LINE], w2_lines(1)[:, split:N // LINE])
+        h_q = hidden(1, [False, True], 2)
+        for b in (0, 2, 1):
+            codes, scales = quantize(woven_w2[:, b * K_PASS:(b + 1) * K_PASS], P, f"w2_1_{b}")
+            second_product(1, b, codes[:], scales[:], h_q, b != 0)
+        scatter(1, 0, 0, C, False)
+        scatter(1, 2, 0, HALF, True)
+        scatter(1, 1, 0, C, True)
+        scatter(1, 2, HALF, HALF, False)
         for b in range(N_BLOCKS):
-            nc.sync.dma_start(out=out[b * P:(b + 1) * P, :], in_=windows[b][:])
+            queue = nc.scalar if b == 1 else nc.sync
+            queue.dma_start(out=out[b * P:(b + 1) * P, :], in_=out_sb[b][:])

@@ -49,10 +49,12 @@ def tile_moe_pre_mlp_relu2_kernel(tc, xT, w1, w2, gate, offs, out):
         x_passes = {g: keep.tile([P, (PACK - 1) * T + WINDOW], F32, name=f"x_pass{g}") for g in range(ROW_PASSES, PASSES)}
         w1_tiles = [keep.tile([P, PACK * H], F32, name=f"w1_raw{i}") for i in range(W1_TILES)]
         w2_raw = [keep.tile([P, PACK * N], F32, name=f"w2_raw{e}") for e in range(E)]
-        out_sb = [keep.tile([P, T], F32, name=f"out_sb{b}") for b in range(N_BLOCKS)]
+        out_sb = {b: keep.tile([P, T], F32, name=f"out_sb{b}") for b in (0, 2)}
         gathered = [keep.tile([P, PACK * SLOTS], F32, name=f"gathered{i}") for i in range(2)]
         gated = keep.tile([P, PACK * C], F32, name="gated")
-        woven_vector = [keep.tile([P, PACK * H], BF16, name=f"woven_vector{i}", align_bytes=64) for i in range(2)]
+        woven_vector = [
+            keep.tile([P, PACK * H], BF16, name=f"woven_vector{i}", tag=f"woven_vector{i}", align_bytes=64) for i in range(2)
+        ]
         woven_shared = [keep.tile([P, PACK * H], BF16, name=f"woven_shared{i}", align_bytes=64) for i in range(3)]
         woven_w2 = keep.tile([P, PACK * N], BF16, name="woven_w2", align_bytes=64)
 
@@ -97,7 +99,6 @@ def tile_moe_pre_mlp_relu2_kernel(tc, xT, w1, w2, gate, offs, out):
             gate_bank[:].rearrange("p (m n) -> p n m", m=per_partition),
         )
         nc.scalar.activation(out_sb[2][:], out_sb[0][:], ACT.Copy)
-        nc.gpsimd.memset(out_sb[1][:], 0.0)
         for g in range(ROW_PASSES, PASSES):
             nc.gpsimd.memset(x_passes[g][:, PACK * T:(PACK - 1) * T + WINDOW], 0.0)
 
@@ -157,11 +158,14 @@ def tile_moe_pre_mlp_relu2_kernel(tc, xT, w1, w2, gate, offs, out):
         def weave_w1(e, g, dst):
             to = dst[:].rearrange("p (u i m j) -> p u m j i", u=2, i=2, j=PACK)
             fro = w1_raw(e, g)[:].rearrange("p (j m u i) -> p u m j i", u=2, i=2, j=PACK)
-            for u in range(2):
-                if w1_half_on_scalar(e, g, u):
-                    nc.scalar.copy(to[:, u], fro[:, u])
+            if w1_half_on_scalar(e, g, 0):
+                nc.scalar.copy(to, fro)
+            else:
+                nc.vector.tensor_copy(to[:, 0], fro[:, 0])
+                if w1_half_on_scalar(e, g, 1):
+                    nc.scalar.copy(to[:, 1], fro[:, 1])
                 else:
-                    nc.vector.tensor_copy(to[:, u], fro[:, u])
+                    nc.vector.tensor_copy(to[:, 1], fro[:, 1])
 
         woven_w2_lines = by_lines(woven_w2[:], "c i j")
 
@@ -291,7 +295,7 @@ def tile_moe_pre_mlp_relu2_kernel(tc, xT, w1, w2, gate, offs, out):
                 for b in range(N_BLOCKS):
                     cols = slice(b * P, (b + 1) * P)
                     second_product(0, b, w2_q[0][:, cols], w2_q[1][:, cols], h_q, True)
-                for b in range(N_BLOCKS):
+                for b in (0, 2):
                     scatter(0, b, 0, C, True)
             before = (step, dst)
         quantize_step(before[0], before[1])
@@ -299,7 +303,11 @@ def tile_moe_pre_mlp_relu2_kernel(tc, xT, w1, w2, gate, offs, out):
         split = W2_GROUPS_ON_VECTOR
         nc.vector.tensor_copy(woven_w2_lines[:, 0:split], w2_lines(1)[:, 0:split])
         nc.scalar.copy(woven_w2_lines[:, split:N // LINE], w2_lines(1)[:, split:N // LINE])
+        last_woven = f"woven_vector{(vector_turn - 1) % len(woven_vector)}"
+        out_sb[1] = keep.tile([P, T], F32, name="out_sb1", tag=last_woven, align_bytes=64)
+        nc.gpsimd.memset(out_sb[1][:], 0.0)
         h_q = hidden(1, [False, True], 2)
+        scatter(0, 1, 0, C, True)
         for b in (0, 2, 1):
             codes, scales = quantize(woven_w2[:, b * K_PASS:(b + 1) * K_PASS], P, f"w2_1_{b}")
             second_product(1, b, codes[:], scales[:], h_q, b != 0)

from contextlib import ExitStack

import concourse.mybir as mybir
from concourse.masks import make_identity

K, T, E, C, H, N = 2560, 640, 2, 256, 512, 384
SLOTS = E * C
FLOPS = 2 * SLOTS * (K * H + H * N)
BYTES = 4 * (K * T + E * K * H + E * H * N + SLOTS + N * T) + 2 * 128 * (SLOTS // 16)

F32 = mybir.dt.float32
BF16 = mybir.dt.bfloat16
U32 = mybir.dt.uint32
U16 = mybir.dt.uint16
U8 = mybir.dt.uint8
FP8X4 = mybir.dt.float8_e4m3fn_x4
ACT = mybir.ActivationFunctionType
ALU = mybir.AluOpType

P = 128
PACK = 4
K_PASS = P * PACK
PASSES = K // K_PASS
LAST = PASSES - 1
HALF = C // 2
N_BLOCKS = N // P
PER_COLUMN = 16
LINE = 4

FUSED_PASSES = 2
ROW_PASSES = 3
WINDOW = 2 * SLOTS
W1_TILES = 8
SCALAR_FROM_HALF = 5
SCALAR_PASS_OF_EXPERT_1 = 1
W2_GROUPS_ON_VECTOR = 48


def tile_moe_pre_mlp_relu2_kernel(tc, xT, w1, w2, gate, offs, out):
    nc = tc.nc
    with ExitStack() as ctx:
        keep = ctx.enter_context(tc.tile_pool(name="keep", bufs=1))
        ring = ctx.enter_context(tc.tile_pool(name="ring", bufs=3))
        psum = ctx.enter_context(tc.psum_pool(name="psum", bufs=1))

        offsets = keep.tile([P, SLOTS // PER_COLUMN], U16, name="offsets")
        gate_sb = keep.tile([P, SLOTS], F32, name="gate_sb")
        x_rows = [[keep.tile([P, T], F32, name=f"x_row{g}_{j}") for j in range(PACK)] for g in range(ROW_PASSES)]
        x_passes = {g: keep.tile([P, (PACK - 1) * T + WINDOW], F32, name=f"x_pass{g}") for g in range(ROW_PASSES, PASSES)}
        w1_tiles = [keep.tile([P, PACK * H], F32, name=f"w1_raw{i}") for i in range(W1_TILES)]
        w2_raw = [keep.tile([P, PACK * N], F32, name=f"w2_raw{e}") for e in range(E)]
        out_sb = {b: keep.tile([P, T], F32, name=f"out_sb{b}") for b in (0, 2)}
        gathered = [keep.tile([P, PACK * SLOTS], F32, name=f"gathered{i}") for i in range(2)]
        gated = keep.tile([P, PACK * C], F32, name="gated")
        woven_vector = [
            keep.tile([P, PACK * H], BF16, name=f"woven_vector{i}", tag=f"woven_vector{i}", align_bytes=64) for i in range(2)
        ]
        woven_shared = [keep.tile([P, PACK * H], BF16, name=f"woven_shared{i}", align_bytes=64) for i in range(3)]
        woven_w2 = keep.tile([P, PACK * N], BF16, name="woven_w2", align_bytes=64)

        def w1_raw(e, g):
            return w1_tiles[(e * PASSES + g) % W1_TILES]

        def load_pass(dst, rows):
            nc.sync.dma_start(out=dst, in_=rows.rearrange("(p j) w -> p (j w)", j=PACK))

        def load_x_row(g, j):
            rows = xT[g * K_PASS:(g + 1) * K_PASS, :].rearrange("(p j) w -> p j w", j=PACK)
            nc.sync.dma_start(out=x_rows[g][j][:], in_=rows[:, j, :])

        def load_w1(e, g):
            load_pass(w1_raw(e, g)[:], w1[e, g * K_PASS:(g + 1) * K_PASS, :])

        per_partition = SLOTS // P
        gate_cols = keep.tile([P, per_partition], F32, name="gate_cols")
        nc.scalar.dma_start(out=gate_cols[:], in_=gate[0:1, :].rearrange("o (n m) -> (o n) m", n=P))
        for g in range(ROW_PASSES):
            for j in range(PACK):
                load_x_row(g, j)
                if (g, j) == (0, 0):
                    nc.sync.dma_start(offsets[:], offs)
        for g in range(PASSES):
            if ROW_PASSES + g < PASSES:
                x_pass = ROW_PASSES + g
                load_pass(x_passes[x_pass][:, 0:PACK * T], xT[x_pass * K_PASS:(x_pass + 1) * K_PASS, :])
            load_w1(0, g)
        load_pass(w2_raw[0][:], w2[0])
        for g in range(W1_TILES - PASSES):
            load_w1(1, g)

        identity = keep.tile([P, P], F32, name="identity")
        nc.gpsimd.memset(out_sb[0][:], 0.0)
        make_identity(nc, identity[:])
        gate_bank = psum.tile([P, SLOTS], F32, name="gate_bank")
        for m in range(per_partition):
            nc.tensor.transpose(gate_bank[:, m * P:(m + 1) * P], gate_cols[:, m:m + 1].to_broadcast([P, P]), identity[:])
        nc.vector.tensor_copy(
            gate_sb[:].rearrange("p (n m) -> p n m", m=per_partition),
            gate_bank[:].rearrange("p (m n) -> p n m", m=per_partition),
        )
        nc.scalar.activation(out_sb[2][:], out_sb[0][:], ACT.Copy)
        for g in range(ROW_PASSES, PASSES):
            nc.gpsimd.memset(x_passes[g][:, PACK * T:(PACK - 1) * T + WINDOW], 0.0)

        def slots(e, first=0, count=C):
            start = (e * C + first) // PER_COLUMN
            return offsets[:, start:start + count // PER_COLUMN]

        def quantize(values, width, name, pool=keep):
            codes = pool.tile([P, width], U32, name=f"{name}_codes", align_bytes=64)
            scales = pool.tile([P, width], U8, name=f"{name}_scales", align_bytes=64)
            nc.vector.quantize_mx(out=codes[:].bitcast(FP8X4), scales=scales[:], in_=values)
            return codes, scales

        def by_lines(ap, order):
            return ap.rearrange(f"p ({order}) -> p c j i", i=LINE, j=PACK)

        def gate_and_weave(src, dst, first, count):
            weight = gate_sb[:, first:first + count].rearrange("p (c i) -> p c i", i=LINE)
            nc.vector.tensor_tensor(
                by_lines(dst, "c i j"),
                src,
                weight.unsqueeze(2).to_broadcast([P, count // LINE, PACK, LINE]),
                ALU.mult,
            )

        def gather_on_scalar(g):
            dst = gathered[g % 2]
            for j in range(PACK):
                if g < FUSED_PASSES:
                    nc.scalar.activation(dst[:, j * C:(j + 1) * C], x_rows[g][j][:].indirect(slots(0)), ACT.Copy)
                else:
                    window = x_rows[g][j][:] if g < ROW_PASSES else x_passes[g][:, j * T:j * T + WINDOW]
                    nc.scalar.activation(dst[:, j * SLOTS:(j + 1) * SLOTS], window.indirect(offsets[:]), ACT.Copy)

        def weave_x(e, g, dst):
            src = gathered[g % 2]
            if g < FUSED_PASSES:
                for j in range(PACK):
                    nc.vector.tensor_tensor(
                        gated[:, j * C:(j + 1) * C], x_rows[g][j][:].indirect(slots(1)), gate_sb[:, C:SLOTS], ALU.mult
                    )
                gate_and_weave(by_lines(src[:, 0:PACK * C], "j c i"), dst[:, 0:PACK * C], 0, C)
                nc.vector.tensor_copy(by_lines(dst[:, PACK * C:PACK * SLOTS], "c i j"), by_lines(gated[:], "j c i"))
            elif g < LAST:
                gate_and_weave(by_lines(src[:], "j c i"), dst[:], 0, SLOTS)
            else:
                groups = slice(e * C // LINE, (e + 1) * C // LINE)
                gate_and_weave(by_lines(src[:], "j c i")[:, groups], dst[:, 0:PACK * C], e * C, C)
            if g + 2 < PASSES:
                gather_on_scalar(g + 2)

        def w1_half_on_scalar(e, g, u):
            if e == 0:
                return 2 * g + u >= SCALAR_FROM_HALF
            return g == SCALAR_PASS_OF_EXPERT_1 and u == 1

        def weave_w1(e, g, dst):
            to = dst[:].rearrange("p (u i m j) -> p u m j i", u=2, i=2, j=PACK)
            fro = w1_raw(e, g)[:].rearrange("p (j m u i) -> p u m j i", u=2, i=2, j=PACK)
            if w1_half_on_scalar(e, g, 0):
                nc.scalar.copy(to, fro)
            else:
                nc.vector.tensor_copy(to[:, 0], fro[:, 0])
                if w1_half_on_scalar(e, g, 1):
                    nc.scalar.copy(to[:, 1], fro[:, 1])
                else:
                    nc.vector.tensor_copy(to[:, 1], fro[:, 1])

        woven_w2_lines = by_lines(woven_w2[:], "c i j")

        def w2_lines(e):
            return by_lines(w2_raw[e][:], "j c i")

        a_banks = [[psum.tile([P, PACK * HALF], F32, name=f"a{e}_{half}") for half in range(2)] for e in range(E)]
        y_sb = [keep.tile([P, N_BLOCKS * C], F32, name=f"y{e}") for e in range(E)]
        x_q = {}

        def first_product(e, g, w_q, tiles):
            x_codes, x_scales, base = x_q[e, g]
            for half in range(2):
                picked = slice(base + half * HALF, base + (half + 1) * HALF)
                for t in tiles:
                    cols = slice((t - tiles.start) * P, (t - tiles.start + 1) * P)
                    nc.tensor.matmul_mx(
                        out=a_banks[e][half][:, t * HALF:(t + 1) * HALF],
                        lhsT=w_q[0][:, cols].bitcast(FP8X4),
                        lhsT_scale=w_q[1][:, cols],
                        rhs=x_codes[:, picked].bitcast(FP8X4),
                        rhs_scale=x_scales[:, picked],
                        start=(g == 0 and t == 0),
                        stop=(g == LAST and t == PACK - 1),
                    )

        def hidden(e, on_scalar, parts):
            codes = keep.tile([P, C], U32, name=f"h{e}_codes", align_bytes=64)
            scales = keep.tile([P, C], U8, name=f"h{e}_scales", align_bytes=64)
            width = HALF // parts
            for half in range(2):
                positive = ring.tile([P, HALF * PACK], F32, name="positive")
                h_bf = ring.tile([P, HALF * PACK], BF16, name="h_bf", align_bytes=64)
                src = a_banks[e][half][:].rearrange("p (t c) -> p c t", t=PACK)
                dst = positive[:].rearrange("p (c t) -> p c t", t=PACK)
                for part in range(parts):
                    part_slots = slice(part * width, (part + 1) * width)
                    if on_scalar[half]:
                        nc.scalar.activation(dst[:, part_slots], src[:, part_slots], ACT.Relu)
                    else:
                        nc.vector.tensor_scalar(dst[:, part_slots], src[:, part_slots], 0.0, None, ALU.max)
                for part in range(parts):
                    values = slice(part * width * PACK, (part + 1) * width * PACK)
                    if on_scalar[half]:
                        nc.scalar.activation(h_bf[:, values], positive[:, values], ACT.Square)
                    else:
                        nc.vector.tensor_tensor(h_bf[:, values], positive[:, values], positive[:, values], ALU.mult)
                cols = slice(half * HALF, (half + 1) * HALF)
                nc.vector.quantize_mx(out=codes[:, cols].bitcast(FP8X4), scales=scales[:, cols], in_=h_bf[:])
            return codes, scales

        def second_product(e, b, w_codes, w_scales, h_q, on_scalar):
            bank = psum.tile([P, C], F32, name=f"y_bank{b}")
            nc.tensor.matmul_mx(
                out=bank[:],
                lhsT=w_codes.bitcast(FP8X4),
                lhsT_scale=w_scales,
                rhs=h_q[0][:].bitcast(FP8X4),
                rhs_scale=h_q[1][:],
                start=True,
                stop=True,
            )
            if on_scalar:
                nc.scalar.copy(y_sb[e][:, b * C:(b + 1) * C], bank[:])
            else:
                nc.vector.tensor_copy(y_sb[e][:, b * C:(b + 1) * C], bank[:])

        def scatter(e, b, first, count, on_scalar):
            target = out_sb[b][:].indirect(slots(e, first, count))
            values = y_sb[e][:, b * C + first:b * C + first + count]
            if on_scalar:
                nc.scalar.activation(target, values, ACT.Copy)
            else:
                nc.vector.tensor_copy(target, values)

        def quantize_step(step, src):
            kind, e, g = step
            if kind == "x" and g < LAST:
                codes, scales = quantize(src[:], SLOTS, f"x{g}")
                for expert in range(E):
                    x_q[expert, g] = (codes, scales, expert * C)
            elif kind == "x":
                codes, scales = quantize(src[:, 0:PACK * C], C, f"x{g}_{e}")
                x_q[e, g] = (codes, scales, 0)
            elif e == 0:
                first_product(e, g, quantize(src[:], H, "w1", ring), range(PACK))
            else:
                for t in range(0, PACK, 2):
                    w_q = quantize(src[:, t * K_PASS:(t + 2) * K_PASS], 2 * P, f"w1_half{t}", ring)
                    first_product(e, g, w_q, range(t, t + 2))

        later_x = [("x", 0, g) for g in range(ROW_PASSES, PASSES)] + [("x", 1, LAST)]
        steps = [("x", 0, g) for g in range(ROW_PASSES)]
        for g in range(PASSES):
            steps.append(("w", 0, g))
            steps.extend(later_x[g:g + 1])
        steps.extend([("w", 1, g) for g in range(PASSES)])

        gather_on_scalar(0)
        gather_on_scalar(1)
        vector_turn = 0
        shared_turn = 0
        before = None
        for step in steps:
            kind, e, g = step
            if kind == "w" and w1_half_on_scalar(e, g, 1):
                dst = woven_shared[shared_turn % len(woven_shared)]
                shared_turn = shared_turn + 1
            else:
                dst = woven_vector[vector_turn % len(woven_vector)]
                vector_turn = vector_turn + 1
            if kind == "w":
                weave_w1(e, g, dst)
            else:
                weave_x(e, g, dst)
            if step == ("w", 0, E * PASSES - W1_TILES - 1):
                for late in range(W1_TILES - PASSES, PASSES):
                    load_w1(1, late)
                load_pass(w2_raw[1][:], w2[1])
            if before is not None:
                quantize_step(before[0], before[1])
            if step == ("w", 1, 0):
                nc.scalar.copy(woven_w2_lines, w2_lines(0))
                w2_q = quantize(woven_w2[:], N, "w2_0")
                h_q = hidden(0, [True, True], 1)
            if step == ("w", 1, SCALAR_PASS_OF_EXPERT_1):
                for b in range(N_BLOCKS):
                    cols = slice(b * P, (b + 1) * P)
                    second_product(0, b, w2_q[0][:, cols], w2_q[1][:, cols], h_q, True)
                for b in (0, 2):
                    scatter(0, b, 0, C, True)
            before = (step, dst)
        quantize_step(before[0], before[1])

        split = W2_GROUPS_ON_VECTOR
        nc.vector.tensor_copy(woven_w2_lines[:, 0:split], w2_lines(1)[:, 0:split])
        nc.scalar.copy(woven_w2_lines[:, split:N // LINE], w2_lines(1)[:, split:N // LINE])
        last_woven = f"woven_vector{(vector_turn - 1) % len(woven_vector)}"
        out_sb[1] = keep.tile([P, T], F32, name="out_sb1", tag=last_woven, align_bytes=64)
        nc.gpsimd.memset(out_sb[1][:], 0.0)
        h_q = hidden(1, [False, True], 2)
        scatter(0, 1, 0, C, True)
        for b in (0, 2, 1):
            codes, scales = quantize(woven_w2[:, b * K_PASS:(b + 1) * K_PASS], P, f"w2_1_{b}")
            second_product(1, b, codes[:], scales[:], h_q, b != 0)
        scatter(1, 0, 0, C, False)
        scatter(1, 2, 0, HALF, True)
        scatter(1, 1, 0, C, True)
        scatter(1, 2, HALF, HALF, False)
        for b in range(N_BLOCKS):
            queue = nc.scalar if b == 1 else nc.sync
            queue.dma_start(out=out[b * P:(b + 1) * P, :], in_=out_sb[b][:])
